import numpy as np, ml_dtypes
CORES = [24,25,26,27,28,29,30,31]
N = 8
BF = ml_dtypes.bfloat16
def f(rng, *shape):
    return (rng.standard_normal(shape, dtype=np.float32) * np.exp2(rng.integers(-2, 3, shape[:-1] + (1,)))).astype(BF)
def wide(rng, *shape):
    v = f(rng, *shape).astype(np.float32); k = shape[:-2] + (1, shape[-1])
    return (v * np.exp2(rng.integers(-6, 7, k)) * (rng.random(k) > 0.0625)).astype(BF)
def gentries(a):
    return np.ascontiguousarray(a.reshape(8, 16, -1).transpose(0, 2, 1)).reshape(8, -1)
def gtable(e):
    e = np.asarray(e); return np.ascontiguousarray(e.reshape(8, -1, 16).transpose(0, 2, 1)).reshape(128, -1).astype(np.int32)
L, K, R, D = 8192, 256, 5, 4095
def corner(rng):
    return rng.integers(0, 4096 - D, (2, 1, 8, 1))
def walk(rng):
    v = np.repeat(rng.integers(-3, 4, (N, 8, L // 64)), 64, axis=2) + rng.integers(-1, 2, (N, 8, L))
    m = (rng.integers(0, D + 1, (N, 8, 1)) + np.add.accumulate(v, axis=2)) % (2 * D)
    return D - np.abs(m - D)
def listeners(rng, o):
    return rng.integers(D, L - 1, (N, 8, K)), o[0] + rng.integers(0, D + 1, (N, 8, K)), o[1] + rng.integers(0, D + 1, (N, 8, K))
def packed(X, Y, s, t, x, z):
    return {"track": (X * 4096 + Y).astype(np.int32), "sound": s, "when": np.stack([gtable(a) for a in t]), "place": np.stack([gtable(a) for a in x * 4096 + z])}
def setup_inputs(rng):
    o = corner(rng); t, x, z = listeners(rng, o)
    return packed(o[0] + walk(rng), o[1] + walk(rng), f(rng, N, 128, L), t, x, z)
def setup_inputs_ends(rng):
    o = np.zeros((2, 1, 8, 1), np.int64); o[:, :, 1::2] = 4095 - D
    X, Y = o[0] + walk(rng), o[1] + walk(rng); t, x, z = listeners(rng, o)
    for g in range(8):
        q = int(rng.integers(0, N)); c = int(o[0, 0, g, 0]); near, far = (c, c + D) if g % 2 == 0 else (c + D, c)
        X[q, g, :D + 1] = near; Y[q, g, :D + 1] = near
        t[:, g, 0] = D; x[:, g, 0] = far; z[:, g, 0] = far
        for r in range(N):
            p = (r + 1) % N; t[r, g, K - 1] = L - 2; x[r, g, K - 1] = X[p, g, L - 2]; z[r, g, K - 1] = Y[p, g, L - 2]
    return packed(X, Y, f(rng, N, 128, L), t, x, z)
def setup_inputs_jumps(rng):
    o = corner(rng); t, x, z = listeners(rng, o)
    return packed(o[0] + rng.integers(0, D + 1, (N, 8, L)), o[1] + rng.integers(0, D + 1, (N, 8, L)), f(rng, N, 128, L), t, x, z)
def setup_inputs_still(rng):
    o = corner(rng); t, x, z = listeners(rng, o); X, Y = o[0] + walk(rng), o[1] + walk(rng)
    q = int(rng.integers(0, N)); r = (q + 1) % N; w = (q + 2) % N
    X[q] = X[q, :, :1].copy(); Y[q] = Y[q, :, :1].copy()
    for a in (t, x, z): a[r, :4] = a[r, :4, :1].copy()
    t[w] = np.sort(t[w], axis=1); x[w] = x[w, :, :1].copy(); z[w] = z[w, :, :1].copy()
    return packed(X, Y, f(rng, N, 128, L), t, x, z)
def setup_inputs_sizes(rng):
    d = np.array([0, 4094, 3, 4000, 64, 3000, 500, 2049]).reshape(1, 8, 1)
    o = rng.integers(0, 4096 - d, (2, 1, 8, 1))
    h = lambda n: rng.integers(0, d + 1, (N, 8, n))
    t = rng.integers(d, L - 1, (N, 8, K)); t[:, 0, 0] = 0
    return packed(o[0] + h(L), o[1] + h(L), f(rng, N, 128, L), t, o[0] + h(K), o[1] + h(K))
def setup_inputs_spread(rng):
    d = setup_inputs(rng); d["sound"] = wide(rng, N, 128, L); return d
def check_inputs(d):
    bad = []; tr = np.asarray(d["track"]).astype(np.int64); pl = np.asarray(d["place"]).astype(np.int64); wh = np.asarray(d["when"]).astype(np.int64)
    if not np.isfinite(np.asarray(d["sound"]).astype(np.float32)).all(): bad.append("finite")
    if tr.min() < 0 or tr.max() >= 4096 * 4096: bad.append("track")
    if pl.min() < 0 or pl.max() >= 4096 * 4096: bad.append("place")
    if wh.min() < 0 or wh.max() > L - 2: bad.append("when")
    ok = True
    for r in range(N):
        t = gentries(wh[r]); w = gentries(pl[r])
        for q in range(N):
            e = np.clip(t, 0, L - 2)
            for i in range(R):
                v = np.take_along_axis(tr[q], e, 1)
                e = t - np.maximum(np.abs((v >> 12) - (w >> 12)), np.abs((v & 4095) - (w & 4095)))
                ok = ok and bool(e.min() >= 0) and bool(e.max() <= L - 2); e = np.clip(e, 0, L - 2)
    if not ok: bad.append("inside")
    return bad
def reference(track, sound, when, place):
    y = np.zeros((N, 128, K), np.float32); s = sound.astype(np.float32).reshape(N, 8, 16, L); tr = track.astype(np.int64)
    for r in range(N):
        t = gentries(when[r]).astype(np.int64); w = gentries(place[r]).astype(np.int64)
        for q in range(N):
            e = t
            for i in range(R):
                v = np.take_along_axis(tr[q], e, 1)
                e = t - np.maximum(np.abs((v >> 12) - (w >> 12)), np.abs((v & 4095) - (w & 4095)))
            u = np.take_along_axis(s[q], e[:, None, :], 2) + np.take_along_axis(s[q], e[:, None, :] + 1, 2)
            y[r] += u.astype(BF).astype(np.float32).reshape(128, K)
    return {"y": y}

@@ -1,0 +1,295 @@
+from concourse.bass import DstId, RemoteDMATransfer
+from concourse.mybir import AluOpType, ActivationFunctionType
+
+N = 8
+R = 5
+L = 8192
+Z1, Z2 = 2944, 5248
+SCRATCH = {
+    "sraw": ("sbuf", [128, 32], "int32"),
+    "si": ("sbuf", [128, 6, 16], "int32"),
+    "land": ("sbuf", [128, 8, 6, 16], "bfloat16"),
+    "cx": ("sbuf", [128, 4, 8, 32], "bfloat16"),
+    "win": ("sbuf", [128, L], "bfloat16"),
+    "snd": ("sbuf", [128, L], "bfloat16"),
+    "trk": ("sbuf", [128, 512], "int32"),
+    "dig": ("sbuf", [128, 4, 512], "int32"),
+    "dgb": ("sbuf", [128, 4, 512], "bfloat16"),
+    "v0": ("sbuf", [128, 1024], "bfloat16"),
+    "v1": ("sbuf", [128, 1024], "bfloat16"),
+    "u0": ("sbuf", [128, 1024], "bfloat16"),
+    "u1": ("sbuf", [128, 1024], "bfloat16"),
+    "a0": ("sbuf", [128, 16, 16], "float32"),
+    "a1": ("sbuf", [128, 16, 16], "float32"),
+    "m0": ("sbuf", [128, 8, 16], "float32"),
+    "m1": ("sbuf", [128, 8, 16], "float32"),
+    "l0": ("sbuf", [128, 64], "uint16"),
+    "l1": ("sbuf", [128, 64], "uint16"),
+    "ul": ("sbuf", [128, 8, 256], "bfloat16"),
+    "ysb": ("sbuf", [128, 256], "float32"),
+    "zb": ("sbuf", [128, 128], "bfloat16"),
+    "i1": ("sbuf", [128, 128], "bfloat16"),
+    "i64": ("sbuf", [128, 128], "bfloat16"),
+    "r16": ("sbuf", [128, 16], "bfloat16"),
+    "qn": ("sbuf", [128, 24, 8], "bfloat16"),
+    "rm": ("sbuf", [128, 64], "float32"),
+    "pi": ("sbuf", [128, 8], "int32"),
+    "mki": ("sbuf", [128, 8], "int32"),
+    "mkf": ("sbuf", [128, 8], "float32"),
+    "p0": ("psum", [128, 64, 8], "float32"),
+    "p1": ("psum", [128, 64, 8], "float32"),
+    "q0": ("psum", [128, 512], "float32"),
+    "q1": ("psum", [128, 512], "float32"),
+    "y0": ("psum", [128, 512], "float32"),
+    "y1": ("psum", [128, 512], "float32"),
+}
+SEMAPHORES = (["vz", "gi", "gk", "gr", "vw", "sz", "va", "vb", "vm", "dl", "dt", "vs", "vl", "vc", "dw", "dn0", "dn1", "ga0", "ga1",
+               "arr", "ls", "lu", "yp0", "yp1", "yc0", "yc1", "dy0", "dy1"]
+              + ["vd%d" % c for c in range(4)] + ["sd%d" % c for c in range(4)]
+              + ["%s%d" % (k, x) for k in ("gv", "gs", "st", "ab", "mx", "tr", "cp", "fv", "fs") for x in range(2)]
+              + ["uq%d" % q for q in range(N)])
+
+
+def rank_program(g, core, T, topo):
+    me = T.rank_of(core)
+    if me is None:
+        return
+    A, F = AluOpType, ActivationFunctionType
+    V, S, P, Y = g.vector, g.scalar, g.tensor, g.sync
+    sem = T.sem
+    AND, SHR = A.bitwise_and, A.logical_shift_right
+
+    def bits(out, in_, shift, mask):
+        if shift and mask:
+            return V.tensor_scalar(out, in_, shift, mask, SHR, AND)
+        if shift:
+            return V.tensor_scalar(out, in_, shift, None, SHR)
+        return V.tensor_scalar(out, in_, mask, None, AND)
+
+    Y.dma_start(T.trk[:], T.track[:]).then_inc(sem.dt, 16)
+    S.dma_start(T.sraw[:, 0:16], T.when[:]).then_inc(sem.dl, 16)
+    S.dma_start(T.sraw[:, 16:32], T.place[:]).then_inc(sem.dl, 16)
+    Y.dma_start(T.snd[:, 0:4096], T.sound[:, 0:4096]).then_inc(sem.dn0, 16)
+
+    V.memset(T.zb[:], 0.0).then_inc(sem.vz, 1)
+    V.memset(T.qn[:, :, :], 0.0).then_inc(sem.vz, 1)
+    V.memset(T.rm[:], -1.0).then_inc(sem.vz, 1)
+    V.memset(T.win[:, 0:Z1], 0.0).then_inc(sem.va, 1)
+    S.wait_ge(sem.va, 1)
+    S.activation(T.win[:, Z2:L], T.win[:, 0:L - Z2], F.Copy).then_inc(sem.sz, 1)
+
+    g.iota(T.pi[:, 0:1], [[1, 1]], 0, 1).then_inc(sem.gi, 1)
+    g.wait_ge(sem.vz, 3)
+    g.affine_select(T.i1[:], T.zb[:], [[-1, 128]], A.not_equal, 1.0, 0, 1).then_inc(sem.gk, 1)
+    g.affine_select(T.i64[:], T.zb[:], [[-1, 128]], A.not_equal, 64.0, 0, 1).then_inc(sem.gk, 1)
+    g.affine_select(T.r16[:], T.zb[:, 0:16], [[-2, 2], [-16, 8]], A.not_equal, 64.0, 0, 1).then_inc(sem.gk, 1)
+    g.affine_select(T.qn[:, 0:8, :], T.qn[:, 0:8, :], [[-16, 8], [-1, 8]], A.not_equal, -64.0, 0, 1).then_inc(sem.gk, 1)
+    g.affine_select(T.qn[:, 16:24, :], T.qn[:, 16:24, :], [[-16, 8], [-1, 8]], A.not_equal, -1.0, 0, 1).then_inc(sem.gk, 1)
+    g.wait_ge(sem.gk, 5)
+    g.affine_select(T.r16[:], T.r16[:], [[-2, 2], [-16, 8]], A.not_equal, 1.0, -1, 1).then_inc(sem.gr, 1)
+    g.affine_select(T.qn[:, 0:8, :], T.qn[:, 0:8, :], [[-16, 8], [-1, 8]], A.not_equal, -64.0, -8, 1).then_inc(sem.gr, 1)
+    g.affine_select(T.qn[:, 16:24, :], T.qn[:, 16:24, :], [[-16, 8], [-1, 8]], A.not_equal, -1.0, -8, 1).then_inc(sem.gr, 1)
+
+    V.wait_ge(sem.gi, 1)
+    bits(T.mki[:, 0:1], T.pi[:, 0:1], 0, 1).then_inc(sem.vb, 1)
+    bits(T.mki[:, 1:2], T.pi[:, 0:1], 3, 1).then_inc(sem.vb, 1)
+    V.wait_ge(sem.vb, 2)
+    V.tensor_scalar(T.mkf[:, 0:2], T.mki[:, 0:2], -1.0, 1.0, A.mult, A.add).then_inc(sem.vm, 1)
+    V.tensor_copy(T.mkf[:, 2:4], T.mki[:, 0:2]).then_inc(sem.vm, 1)
+    V.memset(T.win[:, Z1:Z2], 0.0).then_inc(sem.vw, 1)
+
+    V.wait_ge(sem.dl, 32)
+    t, pl = T.sraw[:, 0:16], T.sraw[:, 16:32]
+    for k, (src, sh, mk) in enumerate(((t, 6, 0), (t, 0, 63), (pl, 18, 0), (pl, 12, 63), (pl, 6, 63), (pl, 0, 63))):
+        bits(T.si[:, k, :], src, sh, mk).then_inc(sem.vs, 1)
+    V.wait_ge(sem.vs, 6)
+    V.tensor_copy(T.land[:, 7, :, :], T.si[:, :, :]).then_inc(sem.vl, 1)
+
+    g.wait_ge(sem.vl, 1)
+    others = [(me + d) % N for d in range(1, N)]
+    dst0 = T.cores[others[0]]
+    mask = topo.mask(core, dst0)
+    neng = len(topo.engines(core, dst0))
+    ids, dsts = [], []
+    for r in others:
+        rid, pid, _ = topo.addr(T.cores[r])
+        ids.append(DstId(rid=rid, pnc=pid))
+        dsts.append(T.land[:, (me - r - 1) % N, :, :])
+    g.remote_dma_fused([RemoteDMATransfer(dst_ids=ids, dma_engine_mask=mask, remote_sem=sem.arr, srcs=[T.land[:, 7, :, :]], dsts=dsts)],
+                       local_sem=sem.ls)
+    g.affine_select(T.rm[:], T.rm[:], [[-2, 64]], A.is_ge, 0.0, 0, 1).then_inc(sem.gr, 1)
+    g.wait_ge(sem.gr, 4)
+    g.affine_select(T.rm[:], T.rm[:], [[2, 64]], A.is_ge, 0.0, 1, -1).then_inc(sem.gr, 1)
+
+    V.wait_ge(sem.dt, 16)
+    Y.wait_ge(sem.va, 1)
+    Y.wait_ge(sem.vw, 1)
+    Y.wait_ge(sem.sz, 1)
+    for c, (sh, mk) in enumerate(((18, 0), (12, 63), (6, 63), (0, 63))):
+        bits(T.dig[:, c, :], T.trk[:], sh, mk).then_inc(sem["vd%d" % c], 1)
+        S.wait_ge(sem["vd%d" % c], 1)
+        S.activation(T.dgb[:, c, :], T.dig[:, c, :], F.Copy).then_inc(sem["sd%d" % c], 1)
+        Y.wait_ge(sem["sd%d" % c], 1)
+        Y.dma_start(T.win[c:128:16, :], T.dgb[:, c, :]).then_inc(sem.dw, 16)
+    Y.dma_start(T.snd[:, 4096:L], T.sound[:, 4096:L]).then_inc(sem.dn1, 16)
+
+    g.wait_ge(sem.dn0, 16)
+    g.wait_ge(sem.dw, 64)
+    g.dma_start(T.snd[:, 0:4096], T.sound[:, 1:4097], accum_op=A.add, max_dma_last_dim=4096).then_inc(sem.ga0, 16)
+    g.wait_ge(sem.dn1, 16)
+    g.dma_start(T.snd[:, 4096:L - 1], T.sound[:, 4097:L], accum_op=A.add, max_dma_last_dim=4096).then_inc(sem.ga1, 16)
+
+    def gather(q, x, tile, win, done):
+        lst, h = T["l%d" % x], (0 if q == "v" else 1)
+        out = T["%s%d" % (tile, x)][:, 512 * h:512 * h + 512]
+        src = win[:, 0:L].indirect(lst[:, 32 * h:32 * h + 32])
+        if q == "v":
+            V.tensor_copy(out, src).then_inc(sem["%sv%d" % (done, x)], 1)
+        else:
+            S.activation(out, src, F.Copy).then_inc(sem["%ss%d" % (done, x)], 1)
+
+    def vgather(x, i):
+        V.wait_ge(sem["cp%d" % x], i + 1)
+        gather("v", x, "v", T.win, "g")
+
+    def sgather(x, i):
+        S.wait_ge(sem["cp%d" % x], i + 1)
+        gather("s", x, "v", T.win, "g")
+
+    def times(x, last):
+        q = T["q%d" % x]
+        P.matmul(q[:, 0:64], T.i64[:], T.land[:, 4 * x:4 * x + 4, 0, :], True, False).then_inc(sem["tr%d" % x], 1)
+        P.matmul(q[:, 0:64], T.i1[:], T.land[:, 4 * x:4 * x + 4, 1, :], False, last).then_inc(sem["tr%d" % x], 1)
+
+    def places(x, i):
+        p, st = T["p%d" % x], sem["st%d" % x]
+        if i:
+            P.wait_ge(sem["ab%d" % x], 2 * i)
+        P.matmul(p[:, 0:16, :], T.cx[:, 0, 4 * x:4 * x + 4, :], T.qn[:, 0:16, :], True, False).then_inc(st, 1)
+        P.matmul(p[:, 0:8, :], T.cx[:, 1, 4 * x:4 * x + 4, :], T.qn[:, 16:24, :], False, False).then_inc(st, 1)
+        P.matmul(p[:, 8:16, :], T.cx[:, 2, 4 * x:4 * x + 4, :], T.qn[:, 0:8, :], False, False).then_inc(st, 1)
+        P.matmul(p[:, 8:16, :], T.cx[:, 3, 4 * x:4 * x + 4, :], T.qn[:, 16:24, :], False, False).then_inc(st, 1)
+
+    def rows(x, i):
+        P.wait_ge(sem["gv%d" % x], i + 1)
+        P.wait_ge(sem["gs%d" % x], i + 1)
+        for b in range(8):
+            P.matmul(T["p%d" % x][:, 0:16, b], T["v%d" % x][:, b:1024:8], T.r16[:], False, b == 7).then_inc(sem["st%d" % x], 1)
+
+    def absolute(x, i):
+        S.wait_ge(sem["st%d" % x], 12 * (i + 1))
+        for h in range(2):
+            S.activation(T["a%d" % x][:, :, 8 * h:8 * h + 8], T["p%d" % x][:, 0:16, :], F.Abs,
+                         scale=T.mkf[:, 2 * h:2 * h + 1]).then_inc(sem["ab%d" % x], 1)
+
+    def larger(x, i):
+        V.wait_ge(sem["ab%d" % x], 2 * (i + 1))
+        a = T["a%d" % x]
+        V.tensor_tensor(T["m%d" % x][:, :, :], a[:, 0:8, :], a[:, 8:16, :], A.max).then_inc(sem["mx%d" % x], 1)
+
+    def back(x, i):
+        P.wait_ge(sem["mx%d" % x], i + 1)
+        P.matmul(T["q%d" % x][:, 0:64], T["m%d" % x][:, :, :], T.rm[:], False, True).then_inc(sem["tr%d" % x], 1)
+
+    def again(x, i):
+        P.wait_ge(sem["cp%d" % x], i + 1)
+        times(x, False)
+
+    def newlist(x, j):
+        V.wait_ge(sem["tr%d" % x], 2 + 3 * j)
+        V.tensor_copy(T["l%d" % x][:], T["q%d" % x][:, 0:64]).then_inc(sem["cp%d" % x], 1)
+
+    P.wait_ge(sem.gk, 5)
+    P.wait_ge(sem.gr, 5)
+    P.wait_ge(sem.vl, 1)
+    P.wait_ge(sem.arr, 7 * neng)
+    times(0, True)
+    times(1, True)
+    newlist(0, 0)
+    newlist(1, 0)
+    V.wait_ge(sem.vm, 2)
+    V.wait_ge(sem.vl, 1)
+    V.wait_ge(sem.arr, 7 * neng)
+    for c in range(4):
+        for h in range(2):
+            V.tensor_scalar(T.cx[:, c, :, h:32:2], T.land[:, :, 2 + c, :], T.mkf[:, 2 * h + 1:2 * h + 2], None, A.mult).then_inc(sem.vc, 1)
+    V.wait_ge(sem.dw, 64)
+    S.wait_ge(sem.dw, 64)
+    S.wait_ge(sem.vm, 2)
+    P.wait_ge(sem.vc, 8)
+
+    for x in range(2):
+        places(x, 0)
+    for i in range(R):
+        vgather(0, i)
+        if i:
+            newlist(1, i)
+        vgather(1, i)
+        larger(0, i)
+        larger(1, i)
+        newlist(0, i + 1)
+        sgather(0, i)
+        sgather(1, i)
+        absolute(0, i)
+        absolute(1, i)
+        rows(0, i)
+        again(0, i)
+        rows(1, i)
+        again(1, i)
+        back(0, i)
+        if i < R - 1:
+            places(0, i + 1)
+        back(1, i)
+        if i < R - 1:
+            places(1, i + 1)
+
+    for q in (V, S):
+        q.wait_ge(sem.ga0, 16)
+        q.wait_ge(sem.ga1, 16)
+    V.wait_ge(sem.cp0, R + 1)
+    gather("v", 0, "u", T.snd, "f")
+    newlist(1, R)
+    V.wait_ge(sem.cp1, R + 1)
+    gather("v", 1, "u", T.snd, "f")
+    for x in range(2):
+        S.wait_ge(sem["cp%d" % x], R + 1)
+        gather("s", x, "u", T.snd, "f")
+    nloc = 0
+    for x in range(2):
+        g.wait_ge(sem["fv%d" % x], 1)
+        g.wait_ge(sem["fs%d" % x], 1)
+        tr = []
+        for s in range(4):
+            r = (me + 1 + 4 * x + s) % N
+            if r == me:
+                continue
+            d = T.cores[r]
+            rid, pid, _ = topo.addr(d)
+            e = topo.engines(core, d)
+            w = len(e) // 4
+            tr.append(RemoteDMATransfer(dst_ids=[DstId(rid=rid, pnc=pid)], dma_engine_mask=sum(1 << k for k in e[w * s:w * s + w]),
+                                        remote_sem=sem["uq%d" % me], srcs=[T["u%d" % x][:, 256 * s:256 * s + 256]], dsts=[T.ul[:, me, :]]))
+            nloc += w
+        g.remote_dma_fused(tr, local_sem=sem.lu)
+
+    for q in range(N):
+        if q == me:
+            P.wait_ge(sem.fv1, 1)
+            P.wait_ge(sem.fs1, 1)
+        else:
+            P.wait_ge(sem["uq%d" % q], len(topo.engines(T.cores[q], core)) // 4)
+        for h in range(2):
+            src = T.u1[:, 768 + 128 * h:896 + 128 * h] if q == me else T.ul[:, q, 128 * h:128 * h + 128]
+            P.matmul(T["y%d" % h][:, 0:128], T.i1[:], src, q == 0, q == N - 1).then_inc(sem["yp%d" % h], 1)
+    V.wait_ge(sem.yp0, N)
+    V.tensor_copy(T.ysb[:, 0:128], T.y0[:, 0:128]).then_inc(sem.yc0, 1)
+    Y.wait_ge(sem.yc0, 1)
+    Y.dma_start(T.y[:, 0:128], T.ysb[:, 0:128]).then_inc(sem.dy0, 16)
+    Y.wait_ge(sem.dy0, 16)
+    S.wait_ge(sem.yp1, N)
+    S.activation(T.ysb[:, 128:256], T.y1[:, 0:128], F.Copy).then_inc(sem.yc1, 1)
+    S.wait_ge(sem.yc1, 1)
+    S.dma_start(T.y[:, 128:256], T.ysb[:, 128:256]).then_inc(sem.dy1, 16)
+    S.wait_ge(sem.dy1, 16)
+    g.wait_ge(sem.ls, neng)
+    g.wait_ge(sem.lu, nloc)

@@ -4,14 +4,20 @@ from concourse.mybir import AluOpType, ActivationFunctionType
 N = 8
 R = 5
 L = 8192
-Z1, Z2 = 2944, 5248
+ZV, ZS = 5632, 512
+VW = 32
+UP = [0, 1, 1, 1, 1, 0, 0]
+H = 512 * sum(UP)
+CUT = 1024
+MID = 5632
 SCRATCH = {
-    "sraw": ("sbuf", [128, 32], "int32"),
-    "si": ("sbuf", [128, 6, 16], "int32"),
-    "land": ("sbuf", [128, 8, 6, 16], "bfloat16"),
-    "cx": ("sbuf", [128, 4, 8, 32], "bfloat16"),
+    "land": ("sbuf", [128, 8, 32], "int32"),
+    "pxy": ("sbuf", [128, 2, 8, 16], "int32"),
+    "cx": ("sbuf", [128, 2, 8, 32], "float16"),
+    "tf": ("sbuf", [128, 8, 16], "float32"),
     "win": ("sbuf", [128, L], "bfloat16"),
-    "snd": ("sbuf", [128, L], "bfloat16"),
+    "snd": ("sbuf", [128, 4608], "bfloat16"),
+    "us": ("sbuf", [128, L], "bfloat16"),
     "trk": ("sbuf", [128, 512], "int32"),
     "dig": ("sbuf", [128, 4, 512], "int32"),
     "dgb": ("sbuf", [128, 4, 512], "bfloat16"),
@@ -21,17 +27,19 @@ SCRATCH = {
     "u1": ("sbuf", [128, 1024], "bfloat16"),
     "a0": ("sbuf", [128, 16, 16], "float32"),
     "a1": ("sbuf", [128, 16, 16], "float32"),
-    "m0": ("sbuf", [128, 8, 16], "float32"),
-    "m1": ("sbuf", [128, 8, 16], "float32"),
     "l0": ("sbuf", [128, 64], "uint16"),
     "l1": ("sbuf", [128, 64], "uint16"),
     "ul": ("sbuf", [128, 8, 256], "bfloat16"),
     "ysb": ("sbuf", [128, 256], "float32"),
     "zb": ("sbuf", [128, 128], "bfloat16"),
     "i1": ("sbuf", [128, 128], "bfloat16"),
-    "i64": ("sbuf", [128, 128], "bfloat16"),
+    "i32": ("sbuf", [128, 128], "float32"),
+    "ec": ("sbuf", [128, 4, 8], "bfloat16"),
+    "es": ("sbuf", [128, 2, 8], "bfloat16"),
     "r16": ("sbuf", [128, 16], "bfloat16"),
-    "qn": ("sbuf", [128, 24, 8], "bfloat16"),
+    "qb": ("sbuf", [128, 2, 64], "bfloat16"),
+    "qn": ("sbuf", [128, 2, 128], "float16"),
+    "rb": ("sbuf", [128, 2, 64], "bfloat16"),
     "rm": ("sbuf", [128, 64], "float32"),
     "pi": ("sbuf", [128, 8], "int32"),
     "mki": ("sbuf", [128, 8], "int32"),
@@ -40,14 +48,18 @@ SCRATCH = {
     "p1": ("psum", [128, 64, 8], "float32"),
     "q0": ("psum", [128, 512], "float32"),
     "q1": ("psum", [128, 512], "float32"),
+    "w0": ("psum", [128, 512], "float32"),
+    "w1": ("psum", [128, 512], "float32"),
     "y0": ("psum", [128, 512], "float32"),
     "y1": ("psum", [128, 512], "float32"),
 }
-SEMAPHORES = (["vz", "gi", "gk", "gr", "vw", "sz", "va", "vb", "vm", "dl", "dt", "vs", "vl", "vc", "dw", "dn0", "dn1", "ga0", "ga1",
-               "arr", "ls", "lu", "yp0", "yp1", "yc0", "yc1", "dy0", "dy1"]
+SEMAPHORES = (["vz", "vy", "gi", "ge", "gq", "gm", "g1", "vb", "vm", "dl", "dt", "vp0", "vp1", "vk", "ve", "vn", "vw", "sz", "dw",
+               "arr", "ls", "lu", "yp0", "yp1", "yc0", "yc1", "dy0", "dy1", "dn0", "dn1", "dn2", "dn3", "ga0", "ga1", "pu", "vu"]
               + ["vd%d" % c for c in range(4)] + ["sd%d" % c for c in range(4)]
-              + ["%s%d" % (k, x) for k in ("gv", "gs", "st", "ab", "mx", "tr", "cp", "fv", "fs") for x in range(2)]
+              + ["%s%d" % (k, x) for k in ("gv", "gs", "st", "ab", "tr", "cp", "fv", "fs") for x in range(2)]
               + ["uq%d" % q for q in range(N)])
+CALLS = [(0, 1, 2, 3), (4, 5), (6,)]
+WIDTH = [4, 4, 4, 4, 2, 2, 1]
 
 
 def rank_program(g, core, T, topo):
@@ -66,46 +78,20 @@ def rank_program(g, core, T, topo):
             return V.tensor_scalar(out, in_, shift, None, SHR)
         return V.tensor_scalar(out, in_, mask, None, AND)
 
+    S.dma_start(T.land[:, 7, 16:32], T.place[:]).then_inc(sem.dl, 16)
+    Y.dma_start(T.land[:, 7, 0:16], T.when[:]).then_inc(sem.dl, 16)
     Y.dma_start(T.trk[:], T.track[:]).then_inc(sem.dt, 16)
-    S.dma_start(T.sraw[:, 0:16], T.when[:]).then_inc(sem.dl, 16)
-    S.dma_start(T.sraw[:, 16:32], T.place[:]).then_inc(sem.dl, 16)
-    Y.dma_start(T.snd[:, 0:4096], T.sound[:, 0:4096]).then_inc(sem.dn0, 16)
+    Y.dma_start(T.snd[:, 0:CUT], T.sound[:, 0:CUT]).then_inc(sem.dn0, 16)
 
+    V.memset(T.win[:, 0:ZS], 0.0).then_inc(sem.vy, 1)
     V.memset(T.zb[:], 0.0).then_inc(sem.vz, 1)
-    V.memset(T.qn[:, :, :], 0.0).then_inc(sem.vz, 1)
-    V.memset(T.rm[:], -1.0).then_inc(sem.vz, 1)
-    V.memset(T.win[:, 0:Z1], 0.0).then_inc(sem.va, 1)
-    S.wait_ge(sem.va, 1)
-    S.activation(T.win[:, Z2:L], T.win[:, 0:L - Z2], F.Copy).then_inc(sem.sz, 1)
+    V.memset(T.win[:, ZS:ZV], 0.0).then_inc(sem.vw, 1)
+    S.wait_ge(sem.vy, 1)
+    for k in range(ZV, L, ZS):
+        S.activation(T.win[:, k:k + ZS], T.win[:, 0:ZS], F.Copy).then_inc(sem.sz, 1)
 
     g.iota(T.pi[:, 0:1], [[1, 1]], 0, 1).then_inc(sem.gi, 1)
-    g.wait_ge(sem.vz, 3)
-    g.affine_select(T.i1[:], T.zb[:], [[-1, 128]], A.not_equal, 1.0, 0, 1).then_inc(sem.gk, 1)
-    g.affine_select(T.i64[:], T.zb[:], [[-1, 128]], A.not_equal, 64.0, 0, 1).then_inc(sem.gk, 1)
-    g.affine_select(T.r16[:], T.zb[:, 0:16], [[-2, 2], [-16, 8]], A.not_equal, 64.0, 0, 1).then_inc(sem.gk, 1)
-    g.affine_select(T.qn[:, 0:8, :], T.qn[:, 0:8, :], [[-16, 8], [-1, 8]], A.not_equal, -64.0, 0, 1).then_inc(sem.gk, 1)
-    g.affine_select(T.qn[:, 16:24, :], T.qn[:, 16:24, :], [[-16, 8], [-1, 8]], A.not_equal, -1.0, 0, 1).then_inc(sem.gk, 1)
-    g.wait_ge(sem.gk, 5)
-    g.affine_select(T.r16[:], T.r16[:], [[-2, 2], [-16, 8]], A.not_equal, 1.0, -1, 1).then_inc(sem.gr, 1)
-    g.affine_select(T.qn[:, 0:8, :], T.qn[:, 0:8, :], [[-16, 8], [-1, 8]], A.not_equal, -64.0, -8, 1).then_inc(sem.gr, 1)
-    g.affine_select(T.qn[:, 16:24, :], T.qn[:, 16:24, :], [[-16, 8], [-1, 8]], A.not_equal, -1.0, -8, 1).then_inc(sem.gr, 1)
-
-    V.wait_ge(sem.gi, 1)
-    bits(T.mki[:, 0:1], T.pi[:, 0:1], 0, 1).then_inc(sem.vb, 1)
-    bits(T.mki[:, 1:2], T.pi[:, 0:1], 3, 1).then_inc(sem.vb, 1)
-    V.wait_ge(sem.vb, 2)
-    V.tensor_scalar(T.mkf[:, 0:2], T.mki[:, 0:2], -1.0, 1.0, A.mult, A.add).then_inc(sem.vm, 1)
-    V.tensor_copy(T.mkf[:, 2:4], T.mki[:, 0:2]).then_inc(sem.vm, 1)
-    V.memset(T.win[:, Z1:Z2], 0.0).then_inc(sem.vw, 1)
-
-    V.wait_ge(sem.dl, 32)
-    t, pl = T.sraw[:, 0:16], T.sraw[:, 16:32]
-    for k, (src, sh, mk) in enumerate(((t, 6, 0), (t, 0, 63), (pl, 18, 0), (pl, 12, 63), (pl, 6, 63), (pl, 0, 63))):
-        bits(T.si[:, k, :], src, sh, mk).then_inc(sem.vs, 1)
-    V.wait_ge(sem.vs, 6)
-    V.tensor_copy(T.land[:, 7, :, :], T.si[:, :, :]).then_inc(sem.vl, 1)
-
-    g.wait_ge(sem.vl, 1)
+    g.wait_ge(sem.vz, 1)
     others = [(me + d) % N for d in range(1, N)]
     dst0 = T.cores[others[0]]
     mask = topo.mask(core, dst0)
@@ -114,61 +100,90 @@ def rank_program(g, core, T, topo):
     for r in others:
         rid, pid, _ = topo.addr(T.cores[r])
         ids.append(DstId(rid=rid, pnc=pid))
-        dsts.append(T.land[:, (me - r - 1) % N, :, :])
-    g.remote_dma_fused([RemoteDMATransfer(dst_ids=ids, dma_engine_mask=mask, remote_sem=sem.arr, srcs=[T.land[:, 7, :, :]], dsts=dsts)],
-                       local_sem=sem.ls)
-    g.affine_select(T.rm[:], T.rm[:], [[-2, 64]], A.is_ge, 0.0, 0, 1).then_inc(sem.gr, 1)
-    g.wait_ge(sem.gr, 4)
-    g.affine_select(T.rm[:], T.rm[:], [[2, 64]], A.is_ge, 0.0, 1, -1).then_inc(sem.gr, 1)
+        dsts.append(T.land[:, (me - r - 1) % N, :])
+    for c in range(4):
+        if c == 2:
+            g.wait_ge(sem.dl, 32)
+            g.remote_dma_fused([RemoteDMATransfer(dst_ids=ids, dma_engine_mask=mask, remote_sem=sem.arr, srcs=[T.land[:, 7, :]], dsts=dsts)],
+                               local_sem=sem.ls)
+        g.affine_select(T.ec[:, c, :], T.zb[:, 0:8], [[-16, 8]], A.not_equal, 1.0 if c % 2 else 64.0, -c, 1).then_inc(sem.ge, 1)
+    for h in range(2):
+        g.affine_select(T.qb[:, h, :], T.zb[:, 0:64], [[-16, 8], [-1, 8]], A.not_equal, -1.0, -8 * h, 1).then_inc(sem.gq, 1)
+    for h in range(2):
+        g.affine_select(T.rb[:, h, :], T.zb[:, 0:64], [[-2, 64]], A.not_equal, -1.0, -h, 1).then_inc(sem.gm, 1)
+    g.affine_select(T.i1[:], T.zb[:], [[-1, 128]], A.not_equal, 1.0, 0, 1).then_inc(sem.g1, 1)
 
     V.wait_ge(sem.dt, 16)
-    Y.wait_ge(sem.va, 1)
+    Y.wait_ge(sem.vy, 1)
     Y.wait_ge(sem.vw, 1)
-    Y.wait_ge(sem.sz, 1)
+    Y.wait_ge(sem.sz, (L - ZV) // ZS)
     for c, (sh, mk) in enumerate(((18, 0), (12, 63), (6, 63), (0, 63))):
         bits(T.dig[:, c, :], T.trk[:], sh, mk).then_inc(sem["vd%d" % c], 1)
         S.wait_ge(sem["vd%d" % c], 1)
-        S.activation(T.dgb[:, c, :], T.dig[:, c, :], F.Copy).then_inc(sem["sd%d" % c], 1)
+        S.activation(T.dgb[:, c, :], T.dig[:, c, :], F.Copy, bias=0.0 if c % 2 else -32.0).then_inc(sem["sd%d" % c], 1)
         Y.wait_ge(sem["sd%d" % c], 1)
         Y.dma_start(T.win[c:128:16, :], T.dgb[:, c, :]).then_inc(sem.dw, 16)
-    Y.dma_start(T.snd[:, 4096:L], T.sound[:, 4096:L]).then_inc(sem.dn1, 16)
-
-    g.wait_ge(sem.dn0, 16)
-    g.wait_ge(sem.dw, 64)
-    g.dma_start(T.snd[:, 0:4096], T.sound[:, 1:4097], accum_op=A.add, max_dma_last_dim=4096).then_inc(sem.ga0, 16)
+    Y.dma_start(T.snd[:, CUT:H + 16], T.sound[:, CUT:H + 16]).then_inc(sem.dn2, 16)
+    Y.dma_start(T.us[:, H:MID], T.sound[:, H:MID]).then_inc(sem.dn1, 16)
+    Y.dma_start(T.us[:, MID:L], T.sound[:, MID:L]).then_inc(sem.dn3, 16)
     g.wait_ge(sem.dn1, 16)
-    g.dma_start(T.snd[:, 4096:L - 1], T.sound[:, 4097:L], accum_op=A.add, max_dma_last_dim=4096).then_inc(sem.ga1, 16)
+    g.dma_start(T.us[:, H:MID], T.sound[:, H + 1:MID + 1], accum_op=A.add, max_dma_last_dim=4096).then_inc(sem.ga0, 16)
+    g.wait_ge(sem.dn3, 16)
+    g.dma_start(T.us[:, MID:L - 1], T.sound[:, MID + 1:L], accum_op=A.add, max_dma_last_dim=4096).then_inc(sem.ga1, 16)
 
-    def gather(q, x, tile, win, done):
-        lst, h = T["l%d" % x], (0 if q == "v" else 1)
-        out = T["%s%d" % (tile, x)][:, 512 * h:512 * h + 512]
-        src = win[:, 0:L].indirect(lst[:, 32 * h:32 * h + 32])
-        if q == "v":
-            V.tensor_copy(out, src).then_inc(sem["%sv%d" % (done, x)], 1)
-        else:
-            S.activation(out, src, F.Copy).then_inc(sem["%ss%d" % (done, x)], 1)
+    V.wait_ge(sem.gi, 1)
+    bits(T.mki[:, 0:1], T.pi[:, 0:1], 3, 1).then_inc(sem.vb, 1)
+    bits(T.mki[:, 1:2], T.pi[:, 0:1], 0, 1).then_inc(sem.vb, 1)
+    V.wait_ge(sem.ge, 4)
+    V.tensor_tensor(T.es[:, :, :], T.ec[:, 0:4:2, :], T.ec[:, 1:4:2, :], A.add).then_inc(sem.ve, 1)
+    V.wait_ge(sem.gq, 2)
+    V.tensor_tensor(T.qn[:, 0, 0:64], T.qb[:, 0, :], T.qb[:, 1, :], A.add).then_inc(sem.vn, 1)
+    V.tensor_tensor(T.qn[:, 0, 64:128], T.qb[:, 0, :], T.qb[:, 1, :], A.add).then_inc(sem.vk, 1)
+    V.tensor_tensor(T.qn[:, 1, 0:64], T.qb[:, 0, :], T.qb[:, 1, :], A.add).then_inc(sem.vk, 1)
+    V.wait_ge(sem.gm, 2)
+    V.tensor_tensor(T.rm[:], T.rb[:, 0, :], T.rb[:, 1, :], A.add).then_inc(sem.vk, 1)
+    V.wait_ge(sem.vb, 2)
+    V.tensor_scalar(T.mkf[:, 0:1], T.mki[:, 0:1], -1.0, 1.0, A.mult, A.add).then_inc(sem.vm, 1)
+    V.tensor_copy(T.mkf[:, 1:2], T.mki[:, 0:1]).then_inc(sem.vm, 1)
+    V.tensor_scalar(T.mkf[:, 2:3], T.mki[:, 1:2], -0.5, 0.5, A.mult, A.add).then_inc(sem.vm, 1)
+    V.tensor_scalar(T.mkf[:, 3:4], T.mki[:, 1:2], 0.5, None, A.mult).then_inc(sem.vm, 1)
+    V.wait_ge(sem.ve, 1)
+    V.tensor_tensor(T.r16[:, 0:8], T.es[:, 0, :], T.es[:, 1, :], A.add).then_inc(sem.vk, 1)
+    V.tensor_tensor(T.r16[:, 8:16], T.es[:, 0, :], T.es[:, 1, :], A.subtract).then_inc(sem.vk, 1)
+    V.wait_ge(sem.vn, 1)
+    V.tensor_scalar(T.qn[:, 1, 64:128], T.qn[:, 0, 0:64], -1.0, None, A.mult).then_inc(sem.vk, 1)
+    V.wait_ge(sem.g1, 1)
+    V.tensor_copy(T.i32[:], T.i1[:]).then_inc(sem.vk, 1)
 
-    def vgather(x, i):
+    def vg(x, i):
         V.wait_ge(sem["cp%d" % x], i + 1)
-        gather("v", x, "v", T.win, "g")
+        V.tensor_copy(T["v%d" % x][:, 0:16 * VW], T.win[:, 0:L].indirect(T["l%d" % x][:, 0:VW])).then_inc(sem["gv%d" % x], 1)
 
-    def sgather(x, i):
+    def sg(x, i):
         S.wait_ge(sem["cp%d" % x], i + 1)
-        gather("s", x, "v", T.win, "g")
+        S.activation(T["v%d" % x][:, 16 * VW:1024], T.win[:, 0:L].indirect(T["l%d" % x][:, VW:64]), F.Copy).then_inc(sem["gs%d" % x], 1)
 
-    def times(x, last):
-        q = T["q%d" % x]
-        P.matmul(q[:, 0:64], T.i64[:], T.land[:, 4 * x:4 * x + 4, 0, :], True, False).then_inc(sem["tr%d" % x], 1)
-        P.matmul(q[:, 0:64], T.i1[:], T.land[:, 4 * x:4 * x + 4, 1, :], False, last).then_inc(sem["tr%d" % x], 1)
+    def prep(x):
+        sl = slice(4 * x, 4 * x + 4)
+        vp = sem["vp%d" % x]
+        bits(T.pxy[:, 0, sl, :], T.land[:, sl, 16:32], 12, 0).then_inc(vp, 1)
+        bits(T.pxy[:, 1, sl, :], T.land[:, sl, 16:32], 0, 4095).then_inc(vp, 1)
+        V.tensor_copy(T.tf[:, sl, :], T.land[:, sl, 0:16]).then_inc(vp, 1)
+        V.wait_ge(vp, 3)
+        for c in range(2):
+            for h in range(2):
+                V.tensor_scalar(T.cx[:, c, sl, h:32:2], T.pxy[:, c, sl, :], -2048.0, T.mkf[:, h:h + 1], A.add, A.mult).then_inc(vp, 1)
+
+    def times(x, i):
+        P.wait_ge(sem["cp%d" % x], i + 1)
+        P.matmul(T["q%d" % x][:, 0:64], T.i32[:], T.tf[:, 4 * x:4 * x + 4, :], True, False).then_inc(sem["tr%d" % x], 1)
 
     def places(x, i):
         p, st = T["p%d" % x], sem["st%d" % x]
         if i:
             P.wait_ge(sem["ab%d" % x], 2 * i)
-        P.matmul(p[:, 0:16, :], T.cx[:, 0, 4 * x:4 * x + 4, :], T.qn[:, 0:16, :], True, False).then_inc(st, 1)
-        P.matmul(p[:, 0:8, :], T.cx[:, 1, 4 * x:4 * x + 4, :], T.qn[:, 16:24, :], False, False).then_inc(st, 1)
-        P.matmul(p[:, 8:16, :], T.cx[:, 2, 4 * x:4 * x + 4, :], T.qn[:, 0:8, :], False, False).then_inc(st, 1)
-        P.matmul(p[:, 8:16, :], T.cx[:, 3, 4 * x:4 * x + 4, :], T.qn[:, 16:24, :], False, False).then_inc(st, 1)
+        for c in range(2):
+            P.matmul(p[:, 0:16, :], T.cx[:, c, 4 * x:4 * x + 4, :], T.qn[:, c, :], c == 0, False).then_inc(st, 1)
 
     def rows(x, i):
         P.wait_ge(sem["gv%d" % x], i + 1)
@@ -177,107 +192,137 @@ def rank_program(g, core, T, topo):
             P.matmul(T["p%d" % x][:, 0:16, b], T["v%d" % x][:, b:1024:8], T.r16[:], False, b == 7).then_inc(sem["st%d" % x], 1)
 
     def absolute(x, i):
-        S.wait_ge(sem["st%d" % x], 12 * (i + 1))
+        S.wait_ge(sem["st%d" % x], 10 * (i + 1))
         for h in range(2):
             S.activation(T["a%d" % x][:, :, 8 * h:8 * h + 8], T["p%d" % x][:, 0:16, :], F.Abs,
-                         scale=T.mkf[:, 2 * h:2 * h + 1]).then_inc(sem["ab%d" % x], 1)
-
-    def larger(x, i):
-        V.wait_ge(sem["ab%d" % x], 2 * (i + 1))
-        a = T["a%d" % x]
-        V.tensor_tensor(T["m%d" % x][:, :, :], a[:, 0:8, :], a[:, 8:16, :], A.max).then_inc(sem["mx%d" % x], 1)
+                         scale=T.mkf[:, 2 + h:3 + h]).then_inc(sem["ab%d" % x], 1)
 
     def back(x, i):
-        P.wait_ge(sem["mx%d" % x], i + 1)
-        P.matmul(T["q%d" % x][:, 0:64], T["m%d" % x][:, :, :], T.rm[:], False, True).then_inc(sem["tr%d" % x], 1)
+        P.wait_ge(sem["ab%d" % x], 2 * (i + 1))
+        for c in range(2):
+            P.matmul(T["q%d" % x][:, 0:64], T["a%d" % x][:, 8 * c:8 * c + 8, :], T.rm[:], False, c == 1).then_inc(sem["tr%d" % x], 1)
 
-    def again(x, i):
-        P.wait_ge(sem["cp%d" % x], i + 1)
-        times(x, False)
-
-    def newlist(x, j):
-        V.wait_ge(sem["tr%d" % x], 2 + 3 * j)
+    def newlist(x, i):
+        V.wait_ge(sem["tr%d" % x], 3 * (i + 1))
         V.tensor_copy(T["l%d" % x][:], T["q%d" % x][:, 0:64]).then_inc(sem["cp%d" % x], 1)
 
-    P.wait_ge(sem.gk, 5)
-    P.wait_ge(sem.gr, 5)
-    P.wait_ge(sem.vl, 1)
-    P.wait_ge(sem.arr, 7 * neng)
-    times(0, True)
-    times(1, True)
-    newlist(0, 0)
-    newlist(1, 0)
-    V.wait_ge(sem.vm, 2)
-    V.wait_ge(sem.vl, 1)
-    V.wait_ge(sem.arr, 7 * neng)
-    for c in range(4):
-        for h in range(2):
-            V.tensor_scalar(T.cx[:, c, :, h:32:2], T.land[:, :, 2 + c, :], T.mkf[:, 2 * h + 1:2 * h + 2], None, A.mult).then_inc(sem.vc, 1)
-    V.wait_ge(sem.dw, 64)
-    S.wait_ge(sem.dw, 64)
-    S.wait_ge(sem.vm, 2)
-    P.wait_ge(sem.vc, 8)
+    npiece, nout = [0], [0]
 
+    def pieces(n):
+        for _ in range(n):
+            k = npiece[0]
+            if k == 0:
+                P.wait_ge(sem.dn0, 16)
+            if 512 * k + 513 > CUT >= 512 * k + 1:
+                P.wait_ge(sem.dn2, 16)
+            if k >= 2:
+                P.wait_ge(sem.vu, k - 1)
+            w = T["w%d" % (k % 2)]
+            P.matmul(w[:], T.i1[:], T.snd[:, 512 * k:512 * k + 512], True, False).then_inc(sem.pu, 1)
+            P.matmul(w[:], T.i1[:], T.snd[:, 512 * k + 1:512 * k + 513], False, True).then_inc(sem.pu, 1)
+            npiece[0] += 1
+
+    def out(n):
+        for _ in range(n):
+            k = nout[0]
+            V.wait_ge(sem.pu, 2 * k + 2)
+            V.tensor_copy(T.us[:, 512 * k:512 * k + 512], T["w%d" % (k % 2)][:]).then_inc(sem.vu, 1)
+            nout[0] += 1
+
+    P.wait_ge(sem.g1, 1)
+    pieces(UP[0])
+    out(UP[0])
+    V.wait_ge(sem.dl, 32)
+    V.wait_ge(sem.arr, 7 * neng)
     for x in range(2):
-        places(x, 0)
+        V.tensor_copy(T["l%d" % x][:], T.land[:, 4 * x:4 * x + 4, 0:16]).then_inc(sem["cp%d" % x], 1)
+    V.wait_ge(sem.vm, 4)
+    prep(0)
+    V.wait_ge(sem.dw, 64)
+    S.wait_ge(sem.vm, 4)
+    S.wait_ge(sem.dw, 64)
+    pieces(UP[1])
+    P.wait_ge(sem.vk, 7)
+
     for i in range(R):
-        vgather(0, i)
+        vg(0, i)
         if i:
-            newlist(1, i)
-        vgather(1, i)
-        larger(0, i)
-        larger(1, i)
-        newlist(0, i + 1)
-        sgather(0, i)
-        sgather(1, i)
+            newlist(1, i - 1)
+        else:
+            prep(1)
+        vg(1, i)
+        out(UP[i + 1])
+        newlist(0, i)
+        sg(0, i)
+        sg(1, i)
         absolute(0, i)
         absolute(1, i)
-        rows(0, i)
-        again(0, i)
+        if i == 0:
+            for x in range(2):
+                P.wait_ge(sem["vp%d" % x], 7)
+                places(x, 0)
+                times(x, 0)
+                if x == 0:
+                    rows(0, 0)
+        else:
+            rows(0, i)
+            times(1, i)
         rows(1, i)
-        again(1, i)
         back(0, i)
-        if i < R - 1:
-            places(0, i + 1)
         back(1, i)
         if i < R - 1:
+            places(0, i + 1)
             places(1, i + 1)
+            pieces(UP[i + 2])
+            times(0, i + 1)
 
-    for q in (V, S):
+    def final(x, q, c0, c1):
+        o, src = T["u%d" % x][:, 16 * c0:16 * c1], T.us[:, 0:L].indirect(T["l%d" % x][:, c0:c1])
+        if q is V:
+            V.tensor_copy(o, src).then_inc(sem["fv%d" % x], 1)
+        else:
+            S.activation(o, src, F.Copy).then_inc(sem["fs%d" % x], 1)
+
+    for q in (S, V):
         q.wait_ge(sem.ga0, 16)
         q.wait_ge(sem.ga1, 16)
-    V.wait_ge(sem.cp0, R + 1)
-    gather("v", 0, "u", T.snd, "f")
-    newlist(1, R)
+        q.wait_ge(sem.vu, sum(UP))
+        q.wait_ge(sem.cp0, R + 1)
+    final(0, V, 0, 32)
+    final(0, S, 32, 64)
+    newlist(1, R - 1)
     V.wait_ge(sem.cp1, R + 1)
-    gather("v", 1, "u", T.snd, "f")
-    for x in range(2):
-        S.wait_ge(sem["cp%d" % x], R + 1)
-        gather("s", x, "u", T.snd, "f")
+    S.wait_ge(sem.cp1, R + 1)
+    final(1, V, 0, 16)
+    final(1, S, 16, 32)
+    final(1, V, 32, 40)
+    final(1, S, 40, 48)
+    final(1, V, 48, 56)
+    final(1, S, 56, 64)
+
     nloc = 0
-    for x in range(2):
-        g.wait_ge(sem["fv%d" % x], 1)
-        g.wait_ge(sem["fs%d" % x], 1)
+    for j, slots in enumerate(CALLS):
+        x = slots[0] // 4
+        g.wait_ge(sem["fv%d" % x], max(j, 1))
+        g.wait_ge(sem["fs%d" % x], max(j, 1))
         tr = []
-        for s in range(4):
-            r = (me + 1 + 4 * x + s) % N
-            if r == me:
-                continue
-            d = T.cores[r]
+        for k, s in enumerate(slots):
+            d = T.cores[(me + 1 + s) % N]
             rid, pid, _ = topo.addr(d)
             e = topo.engines(core, d)
-            w = len(e) // 4
-            tr.append(RemoteDMATransfer(dst_ids=[DstId(rid=rid, pnc=pid)], dma_engine_mask=sum(1 << k for k in e[w * s:w * s + w]),
-                                        remote_sem=sem["uq%d" % me], srcs=[T["u%d" % x][:, 256 * s:256 * s + 256]], dsts=[T.ul[:, me, :]]))
+            w = len(e) // WIDTH[s]
+            tr.append(RemoteDMATransfer(dst_ids=[DstId(rid=rid, pnc=pid)], dma_engine_mask=sum(1 << m for m in e[w * k:w * k + w]),
+                                        remote_sem=sem["uq%d" % me], srcs=[T["u%d" % x][:, 256 * (s % 4):256 * (s % 4) + 256]],
+                                        dsts=[T.ul[:, me, :]]))
             nloc += w
         g.remote_dma_fused(tr, local_sem=sem.lu)
 
     for q in range(N):
         if q == me:
-            P.wait_ge(sem.fv1, 1)
-            P.wait_ge(sem.fs1, 1)
+            P.wait_ge(sem.fv1, 3)
+            P.wait_ge(sem.fs1, 3)
         else:
-            P.wait_ge(sem["uq%d" % q], len(topo.engines(T.cores[q], core)) // 4)
+            P.wait_ge(sem["uq%d" % q], len(topo.engines(T.cores[q], core)) // WIDTH[(me - q - 1) % N])
         for h in range(2):
             src = T.u1[:, 768 + 128 * h:896 + 128 * h] if q == me else T.ul[:, q, 128 * h:128 * h + 128]
             P.matmul(T["y%d" % h][:, 0:128], T.i1[:], src, q == 0, q == N - 1).then_inc(sem["yp%d" % h], 1)

@@ -6,10 +6,13 @@ R = 5
 L = 8192
 ZV, ZS = 5632, 512
 VW = 32
+VM = 20
+VF = 32
 UP = [0, 1, 1, 1, 1, 0, 0]
 H = 512 * sum(UP)
 CUT = 1024
 MID = 5632
+NA = 6
 SCRATCH = {
     "land": ("sbuf", [128, 8, 32], "int32"),
     "pxy": ("sbuf", [128, 2, 8, 16], "int32"),
@@ -37,21 +40,21 @@ SCRATCH = {
     "ec": ("sbuf", [128, 4, 8], "bfloat16"),
     "es": ("sbuf", [128, 2, 8], "bfloat16"),
     "r16": ("sbuf", [128, 16], "bfloat16"),
-    "qb": ("sbuf", [128, 2, 64], "bfloat16"),
-    "qn": ("sbuf", [128, 2, 128], "float16"),
+    "qb": ("sbuf", [128, 2, 2, 32], "bfloat16"),
+    "qn": ("sbuf", [128, 2, 2, 2, 32], "float16"),
     "rb": ("sbuf", [128, 2, 64], "bfloat16"),
     "rm": ("sbuf", [128, 64], "float32"),
     "pi": ("sbuf", [128, 8], "int32"),
     "mki": ("sbuf", [128, 8], "int32"),
     "mkf": ("sbuf", [128, 8], "float32"),
-    "p0": ("psum", [128, 64, 8], "float32"),
-    "p1": ("psum", [128, 64, 8], "float32"),
+    "p00": ("psum", [128, 128, 4], "float32"),
+    "p01": ("psum", [128, 128, 4], "float32"),
+    "p10": ("psum", [128, 128, 4], "float32"),
+    "p11": ("psum", [128, 128, 4], "float32"),
     "q0": ("psum", [128, 512], "float32"),
     "q1": ("psum", [128, 512], "float32"),
     "w0": ("psum", [128, 512], "float32"),
     "w1": ("psum", [128, 512], "float32"),
-    "y0": ("psum", [128, 512], "float32"),
-    "y1": ("psum", [128, 512], "float32"),
 }
 SEMAPHORES = (["vz", "vy", "gi", "ge", "gq", "gm", "g1", "vb", "vm", "dl", "dt", "vp0", "vp1", "vk", "ve", "vn", "vw", "sz", "dw",
                "arr", "ls", "lu", "yp0", "yp1", "yc0", "yc1", "dy0", "dy1", "dn0", "dn1", "dn2", "dn3", "ga0", "ga1", "pu", "vu"]
@@ -108,7 +111,7 @@ def rank_program(g, core, T, topo):
                                local_sem=sem.ls)
         g.affine_select(T.ec[:, c, :], T.zb[:, 0:8], [[-16, 8]], A.not_equal, 1.0 if c % 2 else 64.0, -c, 1).then_inc(sem.ge, 1)
     for h in range(2):
-        g.affine_select(T.qb[:, h, :], T.zb[:, 0:64], [[-16, 8], [-1, 8]], A.not_equal, -1.0, -8 * h, 1).then_inc(sem.gq, 1)
+        g.affine_select(T.qb[:, h, :, :], T.zb[:, 0:64], [[-4, 2], [-16, 8], [-1, 4]], A.not_equal, -1.0, -8 * h, 1).then_inc(sem.gq, 1)
     for h in range(2):
         g.affine_select(T.rb[:, h, :], T.zb[:, 0:64], [[-2, 64]], A.not_equal, -1.0, -h, 1).then_inc(sem.gm, 1)
     g.affine_select(T.i1[:], T.zb[:], [[-1, 128]], A.not_equal, 1.0, 0, 1).then_inc(sem.g1, 1)
@@ -118,10 +121,12 @@ def rank_program(g, core, T, topo):
     Y.wait_ge(sem.vw, 1)
     Y.wait_ge(sem.sz, (L - ZV) // ZS)
     for c, (sh, mk) in enumerate(((18, 0), (12, 63), (6, 63), (0, 63))):
-        bits(T.dig[:, c, :], T.trk[:], sh, mk).then_inc(sem["vd%d" % c], 1)
-        S.wait_ge(sem["vd%d" % c], 1)
-        S.activation(T.dgb[:, c, :], T.dig[:, c, :], F.Copy, bias=0.0 if c % 2 else -32.0).then_inc(sem["sd%d" % c], 1)
-        Y.wait_ge(sem["sd%d" % c], 1)
+        for k in range(2):
+            hf = slice(256 * k, 256 * k + 256)
+            bits(T.dig[:, c, hf], T.trk[:, hf], sh, mk).then_inc(sem["vd%d" % c], 1)
+            S.wait_ge(sem["vd%d" % c], k + 1)
+            S.activation(T.dgb[:, c, hf], T.dig[:, c, hf], F.Copy, bias=0.0 if c % 2 else -32.0).then_inc(sem["sd%d" % c], 1)
+        Y.wait_ge(sem["sd%d" % c], 2)
         Y.dma_start(T.win[c:128:16, :], T.dgb[:, c, :]).then_inc(sem.dw, 16)
     Y.dma_start(T.snd[:, CUT:H + 16], T.sound[:, CUT:H + 16]).then_inc(sem.dn2, 16)
     Y.dma_start(T.us[:, H:MID], T.sound[:, H:MID]).then_inc(sem.dn1, 16)
@@ -137,9 +142,9 @@ def rank_program(g, core, T, topo):
     V.wait_ge(sem.ge, 4)
     V.tensor_tensor(T.es[:, :, :], T.ec[:, 0:4:2, :], T.ec[:, 1:4:2, :], A.add).then_inc(sem.ve, 1)
     V.wait_ge(sem.gq, 2)
-    V.tensor_tensor(T.qn[:, 0, 0:64], T.qb[:, 0, :], T.qb[:, 1, :], A.add).then_inc(sem.vn, 1)
-    V.tensor_tensor(T.qn[:, 0, 64:128], T.qb[:, 0, :], T.qb[:, 1, :], A.add).then_inc(sem.vk, 1)
-    V.tensor_tensor(T.qn[:, 1, 0:64], T.qb[:, 0, :], T.qb[:, 1, :], A.add).then_inc(sem.vk, 1)
+    V.tensor_tensor(T.qn[:, 0, :, 0, :], T.qb[:, 0, :, :], T.qb[:, 1, :, :], A.add).then_inc(sem.vn, 1)
+    V.tensor_tensor(T.qn[:, 0, :, 1, :], T.qb[:, 0, :, :], T.qb[:, 1, :, :], A.add).then_inc(sem.vk, 1)
+    V.tensor_tensor(T.qn[:, 1, :, 0, :], T.qb[:, 0, :, :], T.qb[:, 1, :, :], A.add).then_inc(sem.vk, 1)
     V.wait_ge(sem.gm, 2)
     V.tensor_tensor(T.rm[:], T.rb[:, 0, :], T.rb[:, 1, :], A.add).then_inc(sem.vk, 1)
     V.wait_ge(sem.vb, 2)
@@ -151,13 +156,13 @@ def rank_program(g, core, T, topo):
     V.tensor_tensor(T.r16[:, 0:8], T.es[:, 0, :], T.es[:, 1, :], A.add).then_inc(sem.vk, 1)
     V.tensor_tensor(T.r16[:, 8:16], T.es[:, 0, :], T.es[:, 1, :], A.subtract).then_inc(sem.vk, 1)
     V.wait_ge(sem.vn, 1)
-    V.tensor_scalar(T.qn[:, 1, 64:128], T.qn[:, 0, 0:64], -1.0, None, A.mult).then_inc(sem.vk, 1)
+    V.tensor_scalar(T.qn[:, 1, :, 1, :], T.qn[:, 0, :, 0, :], -1.0, None, A.mult).then_inc(sem.vk, 1)
     V.wait_ge(sem.g1, 1)
     V.tensor_copy(T.i32[:], T.i1[:]).then_inc(sem.vk, 1)
 
-    def vg(x, i):
+    def vg(x, i, c0, c1):
         V.wait_ge(sem["cp%d" % x], i + 1)
-        V.tensor_copy(T["v%d" % x][:, 0:16 * VW], T.win[:, 0:L].indirect(T["l%d" % x][:, 0:VW])).then_inc(sem["gv%d" % x], 1)
+        V.tensor_copy(T["v%d" % x][:, 16 * c0:16 * c1], T.win[:, 0:L].indirect(T["l%d" % x][:, c0:c1])).then_inc(sem["gv%d" % x], 1)
 
     def sg(x, i):
         S.wait_ge(sem["cp%d" % x], i + 1)
@@ -179,27 +184,29 @@ def rank_program(g, core, T, topo):
         P.matmul(T["q%d" % x][:, 0:64], T.i32[:], T.tf[:, 4 * x:4 * x + 4, :], True, False).then_inc(sem["tr%d" % x], 1)
 
     def places(x, i):
-        p, st = T["p%d" % x], sem["st%d" % x]
         if i:
-            P.wait_ge(sem["ab%d" % x], 2 * i)
-        for c in range(2):
-            P.matmul(p[:, 0:16, :], T.cx[:, c, 4 * x:4 * x + 4, :], T.qn[:, c, :], c == 0, False).then_inc(st, 1)
+            P.wait_ge(sem["ab%d" % x], NA * i)
+        for f in range(2):
+            for c in range(2):
+                P.matmul(T["p%d%d" % (x, f)][:, 0:16, :], T.cx[:, c, 4 * x:4 * x + 4, :], T.qn[:, c, f, :, :], c == 0, False).then_inc(sem["st%d" % x], 1)
 
     def rows(x, i):
-        P.wait_ge(sem["gv%d" % x], i + 1)
+        P.wait_ge(sem["gv%d" % x], (2 - x) * (i + 1))
         P.wait_ge(sem["gs%d" % x], i + 1)
         for b in range(8):
-            P.matmul(T["p%d" % x][:, 0:16, b], T["v%d" % x][:, b:1024:8], T.r16[:], False, b == 7).then_inc(sem["st%d" % x], 1)
+            P.matmul(T["p%d%d" % (x, b // 4)][:, 0:16, b % 4], T["v%d" % x][:, b:1024:8], T.r16[:], False, b % 4 == 3).then_inc(sem["st%d" % x], 1)
 
     def absolute(x, i):
-        S.wait_ge(sem["st%d" % x], 10 * (i + 1))
-        for h in range(2):
-            S.activation(T["a%d" % x][:, :, 8 * h:8 * h + 8], T["p%d" % x][:, 0:16, :], F.Abs,
-                         scale=T.mkf[:, 2 + h:3 + h]).then_inc(sem["ab%d" % x], 1)
+        for f in range(2):
+            S.wait_ge(sem["st%d" % x], 12 * i + 8 + 4 * f)
+            for c in ((slice(0, 16),), (slice(0, 8), slice(8, 16)))[f]:
+                for h in range(2):
+                    S.activation(T["a%d" % x][:, c, 8 * h + 4 * f:8 * h + 4 * f + 4], T["p%d%d" % (x, f)][:, c, :], F.Abs,
+                                 scale=T.mkf[:, 2 + h:3 + h]).then_inc(sem["ab%d" % x], 1)
 
     def back(x, i):
-        P.wait_ge(sem["ab%d" % x], 2 * (i + 1))
         for c in range(2):
+            P.wait_ge(sem["ab%d" % x], NA * i + 4 + 2 * c)
             P.matmul(T["q%d" % x][:, 0:64], T["a%d" % x][:, 8 * c:8 * c + 8, :], T.rm[:], False, c == 1).then_inc(sem["tr%d" % x], 1)
 
     def newlist(x, i):
@@ -238,6 +245,7 @@ def rank_program(g, core, T, topo):
         V.tensor_copy(T["l%d" % x][:], T.land[:, 4 * x:4 * x + 4, 0:16]).then_inc(sem["cp%d" % x], 1)
     V.wait_ge(sem.vm, 4)
     prep(0)
+    prep(1)
     V.wait_ge(sem.dw, 64)
     S.wait_ge(sem.vm, 4)
     S.wait_ge(sem.dw, 64)
@@ -245,12 +253,11 @@ def rank_program(g, core, T, topo):
     P.wait_ge(sem.vk, 7)
 
     for i in range(R):
-        vg(0, i)
+        vg(0, i, 0, VM)
         if i:
             newlist(1, i - 1)
-        else:
-            prep(1)
-        vg(1, i)
+        vg(0, i, VM, VW)
+        vg(1, i, 0, VW)
         out(UP[i + 1])
         newlist(0, i)
         sg(0, i)
@@ -262,8 +269,7 @@ def rank_program(g, core, T, topo):
                 P.wait_ge(sem["vp%d" % x], 7)
                 places(x, 0)
                 times(x, 0)
-                if x == 0:
-                    rows(0, 0)
+            rows(0, 0)
         else:
             rows(0, i)
             times(1, i)
@@ -288,8 +294,8 @@ def rank_program(g, core, T, topo):
         q.wait_ge(sem.ga1, 16)
         q.wait_ge(sem.vu, sum(UP))
         q.wait_ge(sem.cp0, R + 1)
-    final(0, V, 0, 32)
-    final(0, S, 32, 64)
+    final(0, V, 0, VF)
+    final(0, S, VF, 64)
     newlist(1, R - 1)
     V.wait_ge(sem.cp1, R + 1)
     S.wait_ge(sem.cp1, R + 1)
@@ -317,6 +323,7 @@ def rank_program(g, core, T, topo):
             nloc += w
         g.remote_dma_fused(tr, local_sem=sem.lu)
 
+    P.wait_ge(sem.vu, sum(UP))
     for q in range(N):
         if q == me:
             P.wait_ge(sem.fv1, 3)
@@ -325,14 +332,14 @@ def rank_program(g, core, T, topo):
             P.wait_ge(sem["uq%d" % q], len(topo.engines(T.cores[q], core)) // WIDTH[(me - q - 1) % N])
         for h in range(2):
             src = T.u1[:, 768 + 128 * h:896 + 128 * h] if q == me else T.ul[:, q, 128 * h:128 * h + 128]
-            P.matmul(T["y%d" % h][:, 0:128], T.i1[:], src, q == 0, q == N - 1).then_inc(sem["yp%d" % h], 1)
+            P.matmul(T["w%d" % h][:, 0:128], T.i1[:], src, q == 0, q == N - 1).then_inc(sem["yp%d" % h], 1)
     V.wait_ge(sem.yp0, N)
-    V.tensor_copy(T.ysb[:, 0:128], T.y0[:, 0:128]).then_inc(sem.yc0, 1)
+    V.tensor_copy(T.ysb[:, 0:128], T.w0[:, 0:128]).then_inc(sem.yc0, 1)
     Y.wait_ge(sem.yc0, 1)
     Y.dma_start(T.y[:, 0:128], T.ysb[:, 0:128]).then_inc(sem.dy0, 16)
     Y.wait_ge(sem.dy0, 16)
     S.wait_ge(sem.yp1, N)
-    S.activation(T.ysb[:, 128:256], T.y1[:, 0:128], F.Copy).then_inc(sem.yc1, 1)
+    S.activation(T.ysb[:, 128:256], T.w1[:, 0:128], F.Copy).then_inc(sem.yc1, 1)
     S.wait_ge(sem.yc1, 1)
     S.dma_start(T.y[:, 128:256], T.ysb[:, 128:256]).then_inc(sem.dy1, 16)
     S.wait_ge(sem.dy1, 16)

from concourse.bass import DstId, RemoteDMATransfer
from concourse.mybir import AluOpType, ActivationFunctionType

N = 8
R = 5
L = 8192
ZV, ZS = 5632, 512
VW = 32
VM = 20
VF = 32
UP = [0, 1, 1, 1, 1, 0, 0]
H = 512 * sum(UP)
CUT = 1024
MID = 5632
NA = 6
SCRATCH = {
    "land": ("sbuf", [128, 8, 32], "int32"),
    "pxy": ("sbuf", [128, 2, 8, 16], "int32"),
    "cx": ("sbuf", [128, 2, 8, 32], "float16"),
    "tf": ("sbuf", [128, 8, 16], "float32"),
    "win": ("sbuf", [128, L], "bfloat16"),
    "snd": ("sbuf", [128, 4608], "bfloat16"),
    "us": ("sbuf", [128, L], "bfloat16"),
    "trk": ("sbuf", [128, 512], "int32"),
    "dig": ("sbuf", [128, 4, 512], "int32"),
    "dgb": ("sbuf", [128, 4, 512], "bfloat16"),
    "v0": ("sbuf", [128, 1024], "bfloat16"),
    "v1": ("sbuf", [128, 1024], "bfloat16"),
    "u0": ("sbuf", [128, 1024], "bfloat16"),
    "u1": ("sbuf", [128, 1024], "bfloat16"),
    "a0": ("sbuf", [128, 16, 16], "float32"),
    "a1": ("sbuf", [128, 16, 16], "float32"),
    "l0": ("sbuf", [128, 64], "uint16"),
    "l1": ("sbuf", [128, 64], "uint16"),
    "ul": ("sbuf", [128, 8, 256], "bfloat16"),
    "ysb": ("sbuf", [128, 256], "float32"),
    "zb": ("sbuf", [128, 128], "bfloat16"),
    "i1": ("sbuf", [128, 128], "bfloat16"),
    "i32": ("sbuf", [128, 128], "float32"),
    "ec": ("sbuf", [128, 4, 8], "bfloat16"),
    "es": ("sbuf", [128, 2, 8], "bfloat16"),
    "r16": ("sbuf", [128, 16], "bfloat16"),
    "qb": ("sbuf", [128, 2, 2, 32], "bfloat16"),
    "qn": ("sbuf", [128, 2, 2, 2, 32], "float16"),
    "rb": ("sbuf", [128, 2, 64], "bfloat16"),
    "rm": ("sbuf", [128, 64], "float32"),
    "pi": ("sbuf", [128, 8], "int32"),
    "mki": ("sbuf", [128, 8], "int32"),
    "mkf": ("sbuf", [128, 8], "float32"),
    "p00": ("psum", [128, 128, 4], "float32"),
    "p01": ("psum", [128, 128, 4], "float32"),
    "p10": ("psum", [128, 128, 4], "float32"),
    "p11": ("psum", [128, 128, 4], "float32"),
    "q0": ("psum", [128, 512], "float32"),
    "q1": ("psum", [128, 512], "float32"),
    "w0": ("psum", [128, 512], "float32"),
    "w1": ("psum", [128, 512], "float32"),
}
SEMAPHORES = (["vz", "vy", "gi", "ge", "gq", "gm", "g1", "vb", "vm", "dl", "dt", "vp0", "vp1", "vk", "ve", "vn", "vw", "sz", "dw",
               "arr", "ls", "lu", "yp0", "yp1", "yc0", "yc1", "dy0", "dy1", "dn0", "dn1", "dn2", "dn3", "ga0", "ga1", "pu", "vu"]
              + ["vd%d" % c for c in range(4)] + ["sd%d" % c for c in range(4)]
              + ["%s%d" % (k, x) for k in ("gv", "gs", "st", "ab", "tr", "cp", "fv", "fs") for x in range(2)]
              + ["uq%d" % q for q in range(N)])
CALLS = [(0, 1, 2, 3), (4, 5), (6,)]
WIDTH = [4, 4, 4, 4, 2, 2, 1]


def rank_program(g, core, T, topo):
    me = T.rank_of(core)
    if me is None:
        return
    A, F = AluOpType, ActivationFunctionType
    V, S, P, Y = g.vector, g.scalar, g.tensor, g.sync
    sem = T.sem
    AND, SHR = A.bitwise_and, A.logical_shift_right

    def bits(out, in_, shift, mask):
        if shift and mask:
            return V.tensor_scalar(out, in_, shift, mask, SHR, AND)
        if shift:
            return V.tensor_scalar(out, in_, shift, None, SHR)
        return V.tensor_scalar(out, in_, mask, None, AND)

    S.dma_start(T.land[:, 7, 16:32], T.place[:]).then_inc(sem.dl, 16)
    Y.dma_start(T.land[:, 7, 0:16], T.when[:]).then_inc(sem.dl, 16)
    Y.dma_start(T.trk[:], T.track[:]).then_inc(sem.dt, 16)
    Y.dma_start(T.snd[:, 0:CUT], T.sound[:, 0:CUT]).then_inc(sem.dn0, 16)

    V.memset(T.win[:, 0:ZS], 0.0).then_inc(sem.vy, 1)
    V.memset(T.zb[:], 0.0).then_inc(sem.vz, 1)
    V.memset(T.win[:, ZS:ZV], 0.0).then_inc(sem.vw, 1)
    S.wait_ge(sem.vy, 1)
    for k in range(ZV, L, ZS):
        S.activation(T.win[:, k:k + ZS], T.win[:, 0:ZS], F.Copy).then_inc(sem.sz, 1)

    g.iota(T.pi[:, 0:1], [[1, 1]], 0, 1).then_inc(sem.gi, 1)
    g.wait_ge(sem.vz, 1)
    others = [(me + d) % N for d in range(1, N)]
    dst0 = T.cores[others[0]]
    mask = topo.mask(core, dst0)
    neng = len(topo.engines(core, dst0))
    ids, dsts = [], []
    for r in others:
        rid, pid, _ = topo.addr(T.cores[r])
        ids.append(DstId(rid=rid, pnc=pid))
        dsts.append(T.land[:, (me - r - 1) % N, :])
    for c in range(4):
        if c == 2:
            g.wait_ge(sem.dl, 32)
            g.remote_dma_fused([RemoteDMATransfer(dst_ids=ids, dma_engine_mask=mask, remote_sem=sem.arr, srcs=[T.land[:, 7, :]], dsts=dsts)],
                               local_sem=sem.ls)
        g.affine_select(T.ec[:, c, :], T.zb[:, 0:8], [[-16, 8]], A.not_equal, 1.0 if c % 2 else 64.0, -c, 1).then_inc(sem.ge, 1)
    for h in range(2):
        g.affine_select(T.qb[:, h, :, :], T.zb[:, 0:64], [[-4, 2], [-16, 8], [-1, 4]], A.not_equal, -1.0, -8 * h, 1).then_inc(sem.gq, 1)
    for h in range(2):
        g.affine_select(T.rb[:, h, :], T.zb[:, 0:64], [[-2, 64]], A.not_equal, -1.0, -h, 1).then_inc(sem.gm, 1)
    g.affine_select(T.i1[:], T.zb[:], [[-1, 128]], A.not_equal, 1.0, 0, 1).then_inc(sem.g1, 1)

    V.wait_ge(sem.dt, 16)
    Y.wait_ge(sem.vy, 1)
    Y.wait_ge(sem.vw, 1)
    Y.wait_ge(sem.sz, (L - ZV) // ZS)
    for c, (sh, mk) in enumerate(((18, 0), (12, 63), (6, 63), (0, 63))):
        for k in range(2):
            hf = slice(256 * k, 256 * k + 256)
            bits(T.dig[:, c, hf], T.trk[:, hf], sh, mk).then_inc(sem["vd%d" % c], 1)
            S.wait_ge(sem["vd%d" % c], k + 1)
            S.activation(T.dgb[:, c, hf], T.dig[:, c, hf], F.Copy, bias=0.0 if c % 2 else -32.0).then_inc(sem["sd%d" % c], 1)
        Y.wait_ge(sem["sd%d" % c], 2)
        Y.dma_start(T.win[c:128:16, :], T.dgb[:, c, :]).then_inc(sem.dw, 16)
    Y.dma_start(T.snd[:, CUT:H + 16], T.sound[:, CUT:H + 16]).then_inc(sem.dn2, 16)
    Y.dma_start(T.us[:, H:MID], T.sound[:, H:MID]).then_inc(sem.dn1, 16)
    Y.dma_start(T.us[:, MID:L], T.sound[:, MID:L]).then_inc(sem.dn3, 16)
    g.wait_ge(sem.dn1, 16)
    g.dma_start(T.us[:, H:MID], T.sound[:, H + 1:MID + 1], accum_op=A.add, max_dma_last_dim=4096).then_inc(sem.ga0, 16)
    g.wait_ge(sem.dn3, 16)
    g.dma_start(T.us[:, MID:L - 1], T.sound[:, MID + 1:L], accum_op=A.add, max_dma_last_dim=4096).then_inc(sem.ga1, 16)

    V.wait_ge(sem.gi, 1)
    bits(T.mki[:, 0:1], T.pi[:, 0:1], 3, 1).then_inc(sem.vb, 1)
    bits(T.mki[:, 1:2], T.pi[:, 0:1], 0, 1).then_inc(sem.vb, 1)
    V.wait_ge(sem.ge, 4)
    V.tensor_tensor(T.es[:, :, :], T.ec[:, 0:4:2, :], T.ec[:, 1:4:2, :], A.add).then_inc(sem.ve, 1)
    V.wait_ge(sem.gq, 2)
    V.tensor_tensor(T.qn[:, 0, :, 0, :], T.qb[:, 0, :, :], T.qb[:, 1, :, :], A.add).then_inc(sem.vn, 1)
    V.tensor_tensor(T.qn[:, 0, :, 1, :], T.qb[:, 0, :, :], T.qb[:, 1, :, :], A.add).then_inc(sem.vk, 1)
    V.tensor_tensor(T.qn[:, 1, :, 0, :], T.qb[:, 0, :, :], T.qb[:, 1, :, :], A.add).then_inc(sem.vk, 1)
    V.wait_ge(sem.gm, 2)
    V.tensor_tensor(T.rm[:], T.rb[:, 0, :], T.rb[:, 1, :], A.add).then_inc(sem.vk, 1)
    V.wait_ge(sem.vb, 2)
    V.tensor_scalar(T.mkf[:, 0:1], T.mki[:, 0:1], -1.0, 1.0, A.mult, A.add).then_inc(sem.vm, 1)
    V.tensor_copy(T.mkf[:, 1:2], T.mki[:, 0:1]).then_inc(sem.vm, 1)
    V.tensor_scalar(T.mkf[:, 2:3], T.mki[:, 1:2], -0.5, 0.5, A.mult, A.add).then_inc(sem.vm, 1)
    V.tensor_scalar(T.mkf[:, 3:4], T.mki[:, 1:2], 0.5, None, A.mult).then_inc(sem.vm, 1)
    V.wait_ge(sem.ve, 1)
    V.tensor_tensor(T.r16[:, 0:8], T.es[:, 0, :], T.es[:, 1, :], A.add).then_inc(sem.vk, 1)
    V.tensor_tensor(T.r16[:, 8:16], T.es[:, 0, :], T.es[:, 1, :], A.subtract).then_inc(sem.vk, 1)
    V.wait_ge(sem.vn, 1)
    V.tensor_scalar(T.qn[:, 1, :, 1, :], T.qn[:, 0, :, 0, :], -1.0, None, A.mult).then_inc(sem.vk, 1)
    V.wait_ge(sem.g1, 1)
    V.tensor_copy(T.i32[:], T.i1[:]).then_inc(sem.vk, 1)

    def vg(x, i, c0, c1):
        V.wait_ge(sem["cp%d" % x], i + 1)
        V.tensor_copy(T["v%d" % x][:, 16 * c0:16 * c1], T.win[:, 0:L].indirect(T["l%d" % x][:, c0:c1])).then_inc(sem["gv%d" % x], 1)

    def sg(x, i):
        S.wait_ge(sem["cp%d" % x], i + 1)
        S.activation(T["v%d" % x][:, 16 * VW:1024], T.win[:, 0:L].indirect(T["l%d" % x][:, VW:64]), F.Copy).then_inc(sem["gs%d" % x], 1)

    def prep(x):
        sl = slice(4 * x, 4 * x + 4)
        vp = sem["vp%d" % x]
        bits(T.pxy[:, 0, sl, :], T.land[:, sl, 16:32], 12, 0).then_inc(vp, 1)
        bits(T.pxy[:, 1, sl, :], T.land[:, sl, 16:32], 0, 4095).then_inc(vp, 1)
        V.tensor_copy(T.tf[:, sl, :], T.land[:, sl, 0:16]).then_inc(vp, 1)
        V.wait_ge(vp, 3)
        for c in range(2):
            for h in range(2):
                V.tensor_scalar(T.cx[:, c, sl, h:32:2], T.pxy[:, c, sl, :], -2048.0, T.mkf[:, h:h + 1], A.add, A.mult).then_inc(vp, 1)

    def times(x, i):
        P.wait_ge(sem["cp%d" % x], i + 1)
        P.matmul(T["q%d" % x][:, 0:64], T.i32[:], T.tf[:, 4 * x:4 * x + 4, :], True, False).then_inc(sem["tr%d" % x], 1)

    def places(x, i):
        if i:
            P.wait_ge(sem["ab%d" % x], NA * i)
        for f in range(2):
            for c in range(2):
                P.matmul(T["p%d%d" % (x, f)][:, 0:16, :], T.cx[:, c, 4 * x:4 * x + 4, :], T.qn[:, c, f, :, :], c == 0, False).then_inc(sem["st%d" % x], 1)

    def rows(x, i):
        P.wait_ge(sem["gv%d" % x], (2 - x) * (i + 1))
        P.wait_ge(sem["gs%d" % x], i + 1)
        for b in range(8):
            P.matmul(T["p%d%d" % (x, b // 4)][:, 0:16, b % 4], T["v%d" % x][:, b:1024:8], T.r16[:], False, b % 4 == 3).then_inc(sem["st%d" % x], 1)

    def absolute(x, i):
        for f in range(2):
            S.wait_ge(sem["st%d" % x], 12 * i + 8 + 4 * f)
            for c in ((slice(0, 16),), (slice(0, 8), slice(8, 16)))[f]:
                for h in range(2):
                    S.activation(T["a%d" % x][:, c, 8 * h + 4 * f:8 * h + 4 * f + 4], T["p%d%d" % (x, f)][:, c, :], F.Abs,
                                 scale=T.mkf[:, 2 + h:3 + h]).then_inc(sem["ab%d" % x], 1)

    def back(x, i):
        for c in range(2):
            P.wait_ge(sem["ab%d" % x], NA * i + 4 + 2 * c)
            P.matmul(T["q%d" % x][:, 0:64], T["a%d" % x][:, 8 * c:8 * c + 8, :], T.rm[:], False, c == 1).then_inc(sem["tr%d" % x], 1)

    def newlist(x, i):
        V.wait_ge(sem["tr%d" % x], 3 * (i + 1))
        V.tensor_copy(T["l%d" % x][:], T["q%d" % x][:, 0:64]).then_inc(sem["cp%d" % x], 1)

    npiece, nout = [0], [0]

    def pieces(n):
        for _ in range(n):
            k = npiece[0]
            if k == 0:
                P.wait_ge(sem.dn0, 16)
            if 512 * k + 513 > CUT >= 512 * k + 1:
                P.wait_ge(sem.dn2, 16)
            if k >= 2:
                P.wait_ge(sem.vu, k - 1)
            w = T["w%d" % (k % 2)]
            P.matmul(w[:], T.i1[:], T.snd[:, 512 * k:512 * k + 512], True, False).then_inc(sem.pu, 1)
            P.matmul(w[:], T.i1[:], T.snd[:, 512 * k + 1:512 * k + 513], False, True).then_inc(sem.pu, 1)
            npiece[0] += 1

    def out(n):
        for _ in range(n):
            k = nout[0]
            V.wait_ge(sem.pu, 2 * k + 2)
            V.tensor_copy(T.us[:, 512 * k:512 * k + 512], T["w%d" % (k % 2)][:]).then_inc(sem.vu, 1)
            nout[0] += 1

    P.wait_ge(sem.g1, 1)
    pieces(UP[0])
    out(UP[0])
    V.wait_ge(sem.dl, 32)
    V.wait_ge(sem.arr, 7 * neng)
    for x in range(2):
        V.tensor_copy(T["l%d" % x][:], T.land[:, 4 * x:4 * x + 4, 0:16]).then_inc(sem["cp%d" % x], 1)
    V.wait_ge(sem.vm, 4)
    prep(0)
    prep(1)
    V.wait_ge(sem.dw, 64)
    S.wait_ge(sem.vm, 4)
    S.wait_ge(sem.dw, 64)
    pieces(UP[1])
    P.wait_ge(sem.vk, 7)

    for i in range(R):
        vg(0, i, 0, VM)
        if i:
            newlist(1, i - 1)
        vg(0, i, VM, VW)
        vg(1, i, 0, VW)
        out(UP[i + 1])
        newlist(0, i)
        sg(0, i)
        sg(1, i)
        absolute(0, i)
        absolute(1, i)
        if i == 0:
            for x in range(2):
                P.wait_ge(sem["vp%d" % x], 7)
                places(x, 0)
                times(x, 0)
            rows(0, 0)
        else:
            rows(0, i)
            times(1, i)
        rows(1, i)
        back(0, i)
        back(1, i)
        if i < R - 1:
            places(0, i + 1)
            places(1, i + 1)
            pieces(UP[i + 2])
            times(0, i + 1)

    def final(x, q, c0, c1):
        o, src = T["u%d" % x][:, 16 * c0:16 * c1], T.us[:, 0:L].indirect(T["l%d" % x][:, c0:c1])
        if q is V:
            V.tensor_copy(o, src).then_inc(sem["fv%d" % x], 1)
        else:
            S.activation(o, src, F.Copy).then_inc(sem["fs%d" % x], 1)

    for q in (S, V):
        q.wait_ge(sem.ga0, 16)
        q.wait_ge(sem.ga1, 16)
        q.wait_ge(sem.vu, sum(UP))
        q.wait_ge(sem.cp0, R + 1)
    final(0, V, 0, VF)
    final(0, S, VF, 64)
    newlist(1, R - 1)
    V.wait_ge(sem.cp1, R + 1)
    S.wait_ge(sem.cp1, R + 1)
    final(1, V, 0, 16)
    final(1, S, 16, 32)
    final(1, V, 32, 40)
    final(1, S, 40, 48)
    final(1, V, 48, 56)
    final(1, S, 56, 64)

    nloc = 0
    for j, slots in enumerate(CALLS):
        x = slots[0] // 4
        g.wait_ge(sem["fv%d" % x], max(j, 1))
        g.wait_ge(sem["fs%d" % x], max(j, 1))
        tr = []
        for k, s in enumerate(slots):
            d = T.cores[(me + 1 + s) % N]
            rid, pid, _ = topo.addr(d)
            e = topo.engines(core, d)
            w = len(e) // WIDTH[s]
            tr.append(RemoteDMATransfer(dst_ids=[DstId(rid=rid, pnc=pid)], dma_engine_mask=sum(1 << m for m in e[w * k:w * k + w]),
                                        remote_sem=sem["uq%d" % me], srcs=[T["u%d" % x][:, 256 * (s % 4):256 * (s % 4) + 256]],
                                        dsts=[T.ul[:, me, :]]))
            nloc += w
        g.remote_dma_fused(tr, local_sem=sem.lu)

    P.wait_ge(sem.vu, sum(UP))
    for q in range(N):
        if q == me:
            P.wait_ge(sem.fv1, 3)
            P.wait_ge(sem.fs1, 3)
        else:
            P.wait_ge(sem["uq%d" % q], len(topo.engines(T.cores[q], core)) // WIDTH[(me - q - 1) % N])
        for h in range(2):
            src = T.u1[:, 768 + 128 * h:896 + 128 * h] if q == me else T.ul[:, q, 128 * h:128 * h + 128]
            P.matmul(T["w%d" % h][:, 0:128], T.i1[:], src, q == 0, q == N - 1).then_inc(sem["yp%d" % h], 1)
    V.wait_ge(sem.yp0, N)
    V.tensor_copy(T.ysb[:, 0:128], T.w0[:, 0:128]).then_inc(sem.yc0, 1)
    Y.wait_ge(sem.yc0, 1)
    Y.dma_start(T.y[:, 0:128], T.ysb[:, 0:128]).then_inc(sem.dy0, 16)
    Y.wait_ge(sem.dy0, 16)
    S.wait_ge(sem.yp1, N)
    S.activation(T.ysb[:, 128:256], T.w1[:, 0:128], F.Copy).then_inc(sem.yc1, 1)
    S.wait_ge(sem.yc1, 1)
    S.dma_start(T.y[:, 128:256], T.ysb[:, 128:256]).then_inc(sem.dy1, 16)
    S.wait_ge(sem.dy1, 16)
    g.wait_ge(sem.ls, neng)
    g.wait_ge(sem.lu, nloc)
